import numpy as np
import ml_dtypes


def mxq(x, axis, fmt="e4m3"):
    dtype, down = {"e4m3": (ml_dtypes.float8_e4m3fn, 7), "e5m2": (ml_dtypes.float8_e5m2, 14)}[fmt]
    v = np.moveaxis(np.asarray(x, np.float32).astype(ml_dtypes.bfloat16).astype(np.float64), axis, -1)
    blocks = v.reshape(v.shape[:-1] + (-1, 32))
    amax = np.abs(blocks).max(-1, keepdims=True)
    byte = np.maximum(np.where(amax > 0, np.frexp(amax)[1] - 1 + 127, 0) - down, 1)
    scale = np.exp2(byte - 127.0)
    codes = (blocks / scale).astype(np.float32).astype(dtype).astype(np.float64)
    return np.moveaxis((codes * scale).reshape(v.shape), -1, axis)


WIDE = False


def mx_kscale(k):
    if not WIDE:
        return np.ones(k)
    levels = np.array([10, -10, 5, -5, 0])
    if k % 512:
        return np.exp2(np.random.permutation(np.resize(levels, k // 32))).repeat(32)
    a = np.empty((k // 512, 16))
    for p in range(k // 512):
        a[p, :8] = np.random.permutation(np.resize(levels, 8))
        for g in range(8):
            far = levels[np.abs(levels - a[p, g]) >= 10]
            a[p, g + 8] = far[np.random.randint(len(far))]
    return np.exp2(a.ravel()).repeat(32)


def f64(x):
    return np.asarray(x).astype(np.float64)


def striped(idx):
    return np.tile(np.asarray(idx).reshape(-1, 16).T, (8, 1)).astype(np.uint16)


def unstriped(offs):
    return offs[:16].T.reshape(-1).astype(np.int64)


B, N, T, D, DV, NQ = 1, 512, 2048, 512, 512, 256


def setup_inputs():
    n = np.random.standard_normal
    idx = np.random.permutation(T)[:B * N]
    s = mx_kscale(D)[:, None]
    u = np.ones(T)
    u[idx] = mx_kscale(B * N)
    r = np.random.uniform(0.5, 2.0, T)
    rk = np.random.uniform(0.5, 2.0, T)
    k = n((D, T)) / s / rk
    v = n((DV, T)) / (u * r)
    return {
        "qT": (n((B, D, NQ)) * s * (0.60 / np.sqrt(D))).astype(np.float32),
        "kT": k.astype(np.float32),
        "vT": v.astype(np.float32),
        "ks": np.tile(rk, (128, 1)).astype(np.float32),
        "vs": np.tile(u * r, (128, 1)).astype(np.float32),
        "offs": striped(idx),
    }


def reference(qT, kT, vT, ks, vs, offs):
    idx = unstriped(offs)
    k = f64(kT)
    v = f64(vT)
    pick = lambda x: x[:, idx].reshape(x.shape[0], B, N).transpose(1, 0, 2)
    q = f64(qT)
    score = mxq(q, 1, "e4m3").transpose(0, 2, 1) @ mxq(pick(k), 1, "e4m3")
    score = score * pick(f64(ks))[:, :1, :]
    m = score.max(-1, keepdims=True)
    p = np.exp(score - m)
    total = p.sum(-1, keepdims=True)
    w = p * pick(f64(vs))[:, :1, :]
    y = mxq(w, 2, "e4m3") @ mxq(pick(v).transpose(0, 2, 1), 1, "e4m3")
    y = y / total
    return y

@@ -1,0 +1,174 @@
+from contextlib import ExitStack
+
+import concourse.mybir as mybir
+from concourse.masks import make_identity
+
+FLOPS = 2 * 2 * 256 * 512 * 512
+BYTES = 4 * (512 * 256 + 2 * 512 * 2048 + 2 * 2048 + 256 * 512) + 2 * 128 * 32
+
+F32 = mybir.dt.float32
+BF16 = mybir.dt.bfloat16
+U32 = mybir.dt.uint32
+U16 = mybir.dt.uint16
+U8 = mybir.dt.uint8
+FP8X4 = mybir.dt.float8_e4m3fn_x4
+MULT = mybir.AluOpType.mult
+MIN = mybir.AluOpType.min
+AXIS_X = mybir.AxisListType.X
+ACT = mybir.ActivationFunctionType
+
+P = 128
+PACK = 4
+T = 2048
+N = 512
+NQ = 256
+DV = 512
+QB = NQ // P
+EB = DV // P
+SB = N // P
+
+
+def tile_attend_mqa_topk_ks_kernel(tc, qT, kT, vT, ks, vs, offs, out):
+    nc = tc.nc
+    with ExitStack() as ctx:
+        keep = ctx.enter_context(tc.tile_pool(name="keep", bufs=1))
+        psum = ctx.enter_context(tc.psum_pool(name="psum", bufs=1))
+
+        offsets = keep.tile([P, N // 16], U16, name="offsets")
+        q_raw = keep.tile([P, PACK, NQ], F32, name="q_raw")
+        k_win = [keep.tile([P, T], F32, name=f"k_win{t}") for t in range(PACK)]
+        v_win = [keep.tile([P, T], F32, name=f"v_win{g}") for g in range(EB)]
+        ks_win = keep.tile([P, T], F32, name="ks_win")
+        vs_win = keep.tile([P, T], F32, name="vs_win")
+
+        nc.sync.dma_start(offsets[:], offs)
+        nc.sync.dma_start(q_raw[:], qT[0].rearrange("(p j) q -> p j q", j=PACK))
+        k_planes = kT.rearrange("(p j) n -> j p n", j=PACK)
+        nc.vector.memset(ks_win[:], 0.0)
+        nc.gpsimd.memset(vs_win[:], 0.0)
+        nc.sync.dma_start(ks_win[0:1, :], ks[0:1, :])
+        nc.sync.dma_start(vs_win[0:1, :], vs[0:1, :])
+        for t in range(PACK):
+            nc.vector.memset(k_win[t][:, 0:PACK], 0.0)
+            nc.sync.dma_start(k_win[t][:], k_planes[t])
+        for g in range(EB):
+            nc.sync.dma_start(v_win[g][:], vT[g * P : (g + 1) * P, :])
+
+        warm = keep.tile([P, 1], F32, name="warm")
+        nc.vector.memset(warm[:], 0.0)
+        nc.scalar.activation(warm[:], warm[:], ACT.Exp)
+
+        ident = keep.tile([P, P], F32, name="ident")
+        make_identity(nc, ident[:])
+
+        q_bf = keep.tile([P, NQ, PACK], BF16, name="q_bf", align_bytes=64)
+        q_codes = keep.tile([P, NQ], U32, name="q_codes", align_bytes=64)
+        q_scales = keep.tile([P, NQ], U8, name="q_scales", align_bytes=64)
+        nc.scalar.copy(q_bf[:], q_raw[:].rearrange("p j q -> p q j"))
+        nc.vector.quantize_mx(q_codes[:].bitcast(FP8X4), q_scales[:], q_bf[:].rearrange("p q j -> p (q j)"))
+
+        ks_row = keep.tile([P, N], F32, name="ks_row")
+        vs_row = keep.tile([P, N], F32, name="vs_row")
+        nks_col = keep.tile([P, SB], F32, name="nks_col")
+        vs_col = keep.tile([P, PACK], F32, name="vs_col")
+        nc.vector.tensor_copy(ks_row[:], ks_win[:].indirect(offsets[:]))
+        ks_t = psum.tile([P, SB, P], F32, name="ks_t", tag="turn", bufs=4)
+        for c in range(SB):
+            nc.tensor.transpose(ks_t[:, c, :], ks_row[:, c * P : (c + 1) * P], ident[:])
+        nc.vector.tensor_scalar(nks_col[:], ks_t[:, :, 0], -1.0, None, MULT)
+        nc.vector.tensor_copy(vs_row[:], vs_win[:].indirect(offsets[:]))
+        vs_t = psum.tile([P, PACK, P], F32, name="vs_t", tag="turn", bufs=4)
+        for t in range(PACK):
+            nc.tensor.transpose(vs_t[:, t, :], vs_row[:, t::PACK], ident[:])
+        nc.vector.tensor_copy(vs_col[:], vs_t[:, :, 0])
+
+        k_bf = keep.tile([P, N, PACK], BF16, name="k_bf", align_bytes=64)
+        k_codes = keep.tile([P, N], U32, name="k_codes", align_bytes=64)
+        k_scales = keep.tile([P, N], U8, name="k_scales", align_bytes=64)
+        for t in range(PACK):
+            nc.vector.tensor_copy(k_bf[:, :, t], k_win[t][:].indirect(offsets[:]))
+        half = N // 2
+        for h in range(2):
+            cols = slice(h * half, (h + 1) * half)
+            nc.vector.quantize_mx(
+                k_codes[:, cols].bitcast(FP8X4), k_scales[:, cols], k_bf[:, cols, :].rearrange("p n j -> p (n j)")
+            )
+
+        a_t = [keep.tile([P, NQ], F32, name=f"a_t{c}") for c in range(SB)]
+        for c in range(SB):
+            cols = slice(c * P, (c + 1) * P)
+            score = psum.tile([P, NQ], F32, name="score", tag="score", bufs=2)
+            nc.tensor.matmul_mx(
+                score[:], k_codes[:, cols].bitcast(FP8X4), k_scales[:, cols], q_codes[:].bitcast(FP8X4), q_scales[:],
+                start=True, stop=True,
+            )
+            nc.scalar.activation(a_t[c][:], score[:], ACT.Copy, scale=nks_col[:, c : c + 1])
+
+        neg_m = keep.tile([P, QB], F32, name="neg_m")
+        total = [keep.tile([P, 1], F32, name=f"total{b}") for b in range(QB)]
+        inv = keep.tile([P, QB], F32, name="inv")
+        w_codes = keep.tile([P, NQ], U32, name="w_codes", align_bytes=64)
+        w_scales = keep.tile([P, NQ], U8, name="w_scales", align_bytes=64)
+        a_q = []
+        for b in range(QB):
+            a_b = psum.tile([P, N], F32, name=f"a_q{b}", tag="turn", bufs=4)
+            for c in range(SB):
+                nc.tensor.transpose(a_b[:, c * P : (c + 1) * P], a_t[c][:, b * P : (b + 1) * P], ident[:])
+            a_q.append(a_b)
+        p_sb = []
+        for b in range(QB):
+            nc.vector.tensor_reduce(neg_m[:, b : b + 1], a_q[b][:], AXIS_X, MIN)
+            p_b = keep.tile([P, PACK, P], F32, name=f"p_sb{b}")
+            nc.scalar.activation(
+                p_b[:], a_q[b][:].rearrange("q (s t) -> q t s", t=PACK), ACT.Exp,
+                bias=neg_m[:, b : b + 1], scale=-1.0, accum_out=total[b][:],
+            )
+            p_sb.append(p_b)
+        for b in range(QB):
+            p_t = psum.tile([P, PACK, P], F32, name=f"p_t{b}", tag="turn", bufs=4)
+            for t in range(PACK):
+                nc.tensor.transpose(p_t[:, t, :], p_sb[b][:, t, :], ident[:])
+            w_bf = keep.tile([P, P, PACK], BF16, name=f"w_bf{b}", align_bytes=64)
+            nc.vector.tensor_tensor(
+                w_bf[:], p_t[:].rearrange("s t q -> s q t"),
+                vs_col[:].unsqueeze(1).to_broadcast([P, P, PACK]), MULT,
+            )
+            cols = slice(b * P, (b + 1) * P)
+            nc.vector.quantize_mx(
+                w_codes[:, cols].bitcast(FP8X4), w_scales[:, cols], w_bf[:].rearrange("s q t -> s (q t)")
+            )
+            nc.vector.reciprocal(inv[:, b : b + 1], total[b][:])
+
+        early = (EB - 1) * P
+        y_early = [psum.tile([P, early], F32, name=f"y_early{b}") for b in range(QB)]
+        for g in range(EB):
+            last = g == EB - 1
+            v_row = keep.tile([P, N], F32, name=f"v_row{g}")
+            nc.vector.tensor_copy(v_row[:], v_win[g][:].indirect(offsets[:]))
+            v_t = psum.tile([P, PACK, P], F32, name=f"v_t{g}", tag="turn", bufs=4)
+            for t in range(PACK):
+                nc.tensor.transpose(v_t[:, t, :], v_row[:, t::PACK], ident[:])
+            v_bf = keep.tile([P, P, PACK], BF16, name=f"v_bf{g}", align_bytes=64)
+            nc.scalar.copy(v_bf[:], v_t[:].rearrange("s t e -> s e t"))
+            v_codes = keep.tile([P, P], U32, name=f"v_codes{g}", align_bytes=64)
+            v_scales = keep.tile([P, P], U8, name=f"v_scales{g}", align_bytes=64)
+            nc.vector.quantize_mx(v_codes[:].bitcast(FP8X4), v_scales[:], v_bf[:].rearrange("s e t -> s (e t)"))
+            y_last = [psum.tile([P, P], F32, name=f"y_last{b}", tag="score", bufs=2) for b in range(QB)] if last else []
+            for b in range(QB):
+                cols = slice(b * P, (b + 1) * P)
+                y = y_last[b][:] if last else y_early[b][:, g * P : (g + 1) * P]
+                nc.tensor.matmul_mx(
+                    y, w_codes[:, cols].bitcast(FP8X4), w_scales[:, cols], v_codes[:].bitcast(FP8X4), v_scales[:],
+                    start=True, stop=True,
+                )
+            if g >= EB - 2:
+                e_cols = slice(early, DV) if last else slice(0, early)
+                for b in range(QB):
+                    y = y_last[b] if last else y_early[b]
+                    y_sb = keep.tile([P, P if last else early], F32, name=f"y_sb{b}_{g}")
+                    if b == 0:
+                        nc.vector.tensor_scalar(y_sb[:], y[:], inv[:, b : b + 1], None, MULT)
+                        nc.sync.dma_start(out[0, b * P : (b + 1) * P, e_cols], y_sb[:])
+                    else:
+                        nc.scalar.activation(y_sb[:], y[:], ACT.Copy, scale=inv[:, b : b + 1])
+                        (nc.scalar if last else nc.sync).dma_start(out[0, b * P : (b + 1) * P, e_cols], y_sb[:])

@@ -25,6 +25,7 @@ NQ = 256
 DV = 512
 QB = NQ // P
 EB = DV // P
+GATE = 8
 SB = N // P
 
 
@@ -41,17 +42,22 @@ def tile_attend_mqa_topk_ks_kernel(tc, qT, kT, vT, ks, vs, offs, out):
         ks_win = keep.tile([P, T], F32, name="ks_win")
         vs_win = keep.tile([P, T], F32, name="vs_win")
 
-        nc.sync.dma_start(offsets[:], offs)
-        nc.sync.dma_start(q_raw[:], qT[0].rearrange("(p j) q -> p j q", j=PACK))
         k_planes = kT.rearrange("(p j) n -> j p n", j=PACK)
-        nc.vector.memset(ks_win[:], 0.0)
-        nc.gpsimd.memset(vs_win[:], 0.0)
-        nc.sync.dma_start(ks_win[0:1, :], ks[0:1, :])
-        nc.sync.dma_start(vs_win[0:1, :], vs[0:1, :])
-        for t in range(PACK):
-            nc.vector.memset(k_win[t][:, 0:PACK], 0.0)
+        nc.sync.dma_start(offsets[:], offs)
+        nc.sync.dma_start(k_win[0][:], k_planes[0])
+        for win, row, split in ((vs_win, vs, 1024), (ks_win, ks, 1280)):
+            nc.vector.memset(win[:, 0:split], 0.0)
+            nc.gpsimd.memset(win[:, split:T], 0.0)
+            nc.scalar.dma_start(win[0:1, :], row[0:1, :])
+        nc.vector.memset(k_win[1][:, 0:GATE], 0.0)
+        nc.sync.dma_start(k_win[1][:], k_planes[1])
+        nc.vector.memset(q_raw[:, 0, 0:GATE], 0.0)
+        nc.sync.dma_start(q_raw[:], qT[0].rearrange("(p j) q -> p j q", j=PACK))
+        for t in range(2, PACK):
+            nc.vector.memset(k_win[t][:, 0:GATE], 0.0)
             nc.sync.dma_start(k_win[t][:], k_planes[t])
         for g in range(EB):
+            nc.vector.memset(v_win[g][:, 0:GATE], 0.0)
             nc.sync.dma_start(v_win[g][:], vT[g * P : (g + 1) * P, :])
 
         warm = keep.tile([P, 1], F32, name="warm")
@@ -61,26 +67,28 @@ def tile_attend_mqa_topk_ks_kernel(tc, qT, kT, vT, ks, vs, offs, out):
         ident = keep.tile([P, P], F32, name="ident")
         make_identity(nc, ident[:])
 
+        banks = [psum.tile([P, PACK, P], F32, name=f"bank{i}") for i in range(4)]
+
+        rows = keep.tile([P, 2, N], F32, name="rows")
+        ks_row, vs_row = rows[:, 0, :], rows[:, 1, :]
+        nks_col = keep.tile([P, SB], F32, name="nks_col")
+        vs_col = keep.tile([P, PACK], F32, name="vs_col")
+        nc.vector.tensor_copy(vs_row, vs_win[:].indirect(offsets[:]))
+        vs_t = banks[1]
+        for t in range(PACK):
+            nc.tensor.transpose(vs_t[:, t, :], vs_row[:, t::PACK], ident[:])
+        nc.vector.tensor_copy(vs_col[:], vs_t[:, :, 0])
+        nc.vector.tensor_copy(ks_row, ks_win[:].indirect(offsets[:]))
+        ks_t = banks[0]
+        for c in range(SB):
+            nc.tensor.transpose(ks_t[:, c, :], ks_row[:, c * P : (c + 1) * P], ident[:])
+        nc.vector.tensor_scalar(nks_col[:], ks_t[:, :, 0], -1.0, None, MULT)
+
         q_bf = keep.tile([P, NQ, PACK], BF16, name="q_bf", align_bytes=64)
         q_codes = keep.tile([P, NQ], U32, name="q_codes", align_bytes=64)
         q_scales = keep.tile([P, NQ], U8, name="q_scales", align_bytes=64)
         nc.scalar.copy(q_bf[:], q_raw[:].rearrange("p j q -> p q j"))
         nc.vector.quantize_mx(q_codes[:].bitcast(FP8X4), q_scales[:], q_bf[:].rearrange("p q j -> p (q j)"))
-
-        ks_row = keep.tile([P, N], F32, name="ks_row")
-        vs_row = keep.tile([P, N], F32, name="vs_row")
-        nks_col = keep.tile([P, SB], F32, name="nks_col")
-        vs_col = keep.tile([P, PACK], F32, name="vs_col")
-        nc.vector.tensor_copy(ks_row[:], ks_win[:].indirect(offsets[:]))
-        ks_t = psum.tile([P, SB, P], F32, name="ks_t", tag="turn", bufs=4)
-        for c in range(SB):
-            nc.tensor.transpose(ks_t[:, c, :], ks_row[:, c * P : (c + 1) * P], ident[:])
-        nc.vector.tensor_scalar(nks_col[:], ks_t[:, :, 0], -1.0, None, MULT)
-        nc.vector.tensor_copy(vs_row[:], vs_win[:].indirect(offsets[:]))
-        vs_t = psum.tile([P, PACK, P], F32, name="vs_t", tag="turn", bufs=4)
-        for t in range(PACK):
-            nc.tensor.transpose(vs_t[:, t, :], vs_row[:, t::PACK], ident[:])
-        nc.vector.tensor_copy(vs_col[:], vs_t[:, :, 0])
 
         k_bf = keep.tile([P, N, PACK], BF16, name="k_bf", align_bytes=64)
         k_codes = keep.tile([P, N], U32, name="k_codes", align_bytes=64)
@@ -94,15 +102,15 @@ def tile_attend_mqa_topk_ks_kernel(tc, qT, kT, vT, ks, vs, offs, out):
                 k_codes[:, cols].bitcast(FP8X4), k_scales[:, cols], k_bf[:, cols, :].rearrange("p n j -> p (n j)")
             )
 
-        a_t = [keep.tile([P, NQ], F32, name=f"a_t{c}") for c in range(SB)]
+        a_t = keep.tile([P, SB, NQ], F32, name="a_t")
         for c in range(SB):
             cols = slice(c * P, (c + 1) * P)
-            score = psum.tile([P, NQ], F32, name="score", tag="score", bufs=2)
+            score = psum.tile([P, NQ], F32, name=f"score{c}", tag=f"sum{c}")
             nc.tensor.matmul_mx(
                 score[:], k_codes[:, cols].bitcast(FP8X4), k_scales[:, cols], q_codes[:].bitcast(FP8X4), q_scales[:],
                 start=True, stop=True,
             )
-            nc.scalar.activation(a_t[c][:], score[:], ACT.Copy, scale=nks_col[:, c : c + 1])
+            nc.scalar.activation(a_t[:, c, :], score[:], ACT.Copy, scale=nks_col[:, c : c + 1])
 
         neg_m = keep.tile([P, QB], F32, name="neg_m")
         total = [keep.tile([P, 1], F32, name=f"total{b}") for b in range(QB)]
@@ -111,21 +119,21 @@ def tile_attend_mqa_topk_ks_kernel(tc, qT, kT, vT, ks, vs, offs, out):
         w_scales = keep.tile([P, NQ], U8, name="w_scales", align_bytes=64)
         a_q = []
         for b in range(QB):
-            a_b = psum.tile([P, N], F32, name=f"a_q{b}", tag="turn", bufs=4)
+            a_b = banks[b]
             for c in range(SB):
-                nc.tensor.transpose(a_b[:, c * P : (c + 1) * P], a_t[c][:, b * P : (b + 1) * P], ident[:])
+                nc.tensor.transpose(a_b[:, c, :], a_t[:, c, b * P : (b + 1) * P], ident[:])
             a_q.append(a_b)
         p_sb = []
         for b in range(QB):
-            nc.vector.tensor_reduce(neg_m[:, b : b + 1], a_q[b][:], AXIS_X, MIN)
+            nc.vector.tensor_reduce(neg_m[:, b : b + 1], a_q[b][:].rearrange("q c s -> q (c s)"), AXIS_X, MIN)
             p_b = keep.tile([P, PACK, P], F32, name=f"p_sb{b}")
             nc.scalar.activation(
-                p_b[:], a_q[b][:].rearrange("q (s t) -> q t s", t=PACK), ACT.Exp,
+                p_b[:], a_q[b][:].rearrange("q c s -> q (c s)").rearrange("q (s t) -> q t s", t=PACK), ACT.Exp,
                 bias=neg_m[:, b : b + 1], scale=-1.0, accum_out=total[b][:],
             )
             p_sb.append(p_b)
         for b in range(QB):
-            p_t = psum.tile([P, PACK, P], F32, name=f"p_t{b}", tag="turn", bufs=4)
+            p_t = banks[b + 2]
             for t in range(PACK):
                 nc.tensor.transpose(p_t[:, t, :], p_sb[b][:, t, :], ident[:])
             w_bf = keep.tile([P, P, PACK], BF16, name=f"w_bf{b}", align_bytes=64)
@@ -140,12 +148,20 @@ def tile_attend_mqa_topk_ks_kernel(tc, qT, kT, vT, ks, vs, offs, out):
             nc.vector.reciprocal(inv[:, b : b + 1], total[b][:])
 
         early = (EB - 1) * P
-        y_early = [psum.tile([P, early], F32, name=f"y_early{b}") for b in range(QB)]
+        v_row0 = keep.tile([P, N], F32, name="v_row0")
+        v_rows = [
+            v_row0[:],
+            a_t[:, 2:4, :].rearrange("s c q -> s (c q)"),
+            p_sb[1][:].rearrange("q t s -> q (t s)"),
+            p_sb[0][:].rearrange("q t s -> q (t s)"),
+        ]
+        y_early = [psum.tile([P, early], F32, name=f"y_early{b}", tag=f"sum{b}") for b in range(QB)]
+        for g in range(EB):
+            nc.vector.tensor_copy(v_rows[g], v_win[g][:].indirect(offsets[:]))
         for g in range(EB):
             last = g == EB - 1
-            v_row = keep.tile([P, N], F32, name=f"v_row{g}")
-            nc.vector.tensor_copy(v_row[:], v_win[g][:].indirect(offsets[:]))
-            v_t = psum.tile([P, PACK, P], F32, name=f"v_t{g}", tag="turn", bufs=4)
+            v_row = v_rows[g]
+            v_t = banks[(g + 2) % 4]
             for t in range(PACK):
                 nc.tensor.transpose(v_t[:, t, :], v_row[:, t::PACK], ident[:])
             v_bf = keep.tile([P, P, PACK], BF16, name=f"v_bf{g}", align_bytes=64)
@@ -153,7 +169,7 @@ def tile_attend_mqa_topk_ks_kernel(tc, qT, kT, vT, ks, vs, offs, out):
             v_codes = keep.tile([P, P], U32, name=f"v_codes{g}", align_bytes=64)
             v_scales = keep.tile([P, P], U8, name=f"v_scales{g}", align_bytes=64)
             nc.vector.quantize_mx(v_codes[:].bitcast(FP8X4), v_scales[:], v_bf[:].rearrange("s e t -> s (e t)"))
-            y_last = [psum.tile([P, P], F32, name=f"y_last{b}", tag="score", bufs=2) for b in range(QB)] if last else []
+            y_last = [psum.tile([P, P], F32, name=f"y_last{b}", tag=f"sum{b + 2}") for b in range(QB)] if last else []
             for b in range(QB):
                 cols = slice(b * P, (b + 1) * P)
                 y = y_last[b][:] if last else y_early[b][:, g * P : (g + 1) * P]

@@ -53,12 +53,12 @@ def tile_attend_mqa_topk_ks_kernel(tc, qT, kT, vT, ks, vs, offs, out):
         nc.sync.dma_start(k_win[1][:], k_planes[1])
         nc.vector.memset(q_raw[:, 0, 0:GATE], 0.0)
         nc.sync.dma_start(q_raw[:], qT[0].rearrange("(p j) q -> p j q", j=PACK))
-        for t in range(2, PACK):
-            nc.vector.memset(k_win[t][:, 0:GATE], 0.0)
-            nc.sync.dma_start(k_win[t][:], k_planes[t])
-        for g in range(EB):
-            nc.vector.memset(v_win[g][:, 0:GATE], 0.0)
-            nc.sync.dma_start(v_win[g][:], vT[g * P : (g + 1) * P, :])
+        v_planes = vT.rearrange("(g e) n -> g e n", e=P)
+        pool_loads = [(k_win[2], k_planes[2]), (v_win[0], v_planes[0]), (k_win[3], k_planes[3])]
+        pool_loads += [(v_win[g], v_planes[g]) for g in range(1, EB)]
+        for win, plane in pool_loads:
+            nc.vector.memset(win[:, 0:GATE], 0.0)
+            nc.sync.dma_start(win[:], plane)
 
         warm = keep.tile([P, 1], F32, name="warm")
         nc.vector.memset(warm[:], 0.0)
@@ -93,8 +93,23 @@ def tile_attend_mqa_topk_ks_kernel(tc, qT, kT, vT, ks, vs, offs, out):
         k_bf = keep.tile([P, N, PACK], BF16, name="k_bf", align_bytes=64)
         k_codes = keep.tile([P, N], U32, name="k_codes", align_bytes=64)
         k_scales = keep.tile([P, N], U8, name="k_scales", align_bytes=64)
-        for t in range(PACK):
+        for t in range(PACK - 1):
             nc.vector.tensor_copy(k_bf[:, :, t], k_win[t][:].indirect(offsets[:]))
+
+        v_bf = [keep.tile([P, 2 * P, PACK], BF16, name=f"v_bf{h}", align_bytes=64) for h in range(2)]
+        v_row0 = keep.tile([P, N], F32, name="v_row0")
+
+        def turn_values(g, row):
+            v_t = banks[(g + 2) % 4]
+            for t in range(PACK):
+                nc.tensor.transpose(v_t[:, t, :], row[:, t::PACK], ident[:])
+            e_cols = slice((g % 2) * P, (g % 2 + 1) * P)
+            nc.scalar.copy(v_bf[g // 2][:, e_cols, :], v_t[:].rearrange("s t e -> s e t"))
+
+        nc.vector.tensor_copy(v_row0[:], v_win[0][:].indirect(offsets[:]))
+        turn_values(0, v_row0)
+
+        nc.vector.tensor_copy(k_bf[:, :, PACK - 1], k_win[PACK - 1][:].indirect(offsets[:]))
         half = N // 2
         for h in range(2):
             cols = slice(h * half, (h + 1) * half)
@@ -147,44 +162,32 @@ def tile_attend_mqa_topk_ks_kernel(tc, qT, kT, vT, ks, vs, offs, out):
             )
             nc.vector.reciprocal(inv[:, b : b + 1], total[b][:])
 
-        early = (EB - 1) * P
-        v_row0 = keep.tile([P, N], F32, name="v_row0")
         v_rows = [
             v_row0[:],
             a_t[:, 2:4, :].rearrange("s c q -> s (c q)"),
             p_sb[1][:].rearrange("q t s -> q (t s)"),
             p_sb[0][:].rearrange("q t s -> q (t s)"),
         ]
-        y_early = [psum.tile([P, early], F32, name=f"y_early{b}", tag=f"sum{b}") for b in range(QB)]
-        for g in range(EB):
+        for g in range(1, EB):
             nc.vector.tensor_copy(v_rows[g], v_win[g][:].indirect(offsets[:]))
-        for g in range(EB):
-            last = g == EB - 1
-            v_row = v_rows[g]
-            v_t = banks[(g + 2) % 4]
-            for t in range(PACK):
-                nc.tensor.transpose(v_t[:, t, :], v_row[:, t::PACK], ident[:])
-            v_bf = keep.tile([P, P, PACK], BF16, name=f"v_bf{g}", align_bytes=64)
-            nc.scalar.copy(v_bf[:], v_t[:].rearrange("s t e -> s e t"))
-            v_codes = keep.tile([P, P], U32, name=f"v_codes{g}", align_bytes=64)
-            v_scales = keep.tile([P, P], U8, name=f"v_scales{g}", align_bytes=64)
-            nc.vector.quantize_mx(v_codes[:].bitcast(FP8X4), v_scales[:], v_bf[:].rearrange("s e t -> s (e t)"))
-            y_last = [psum.tile([P, P], F32, name=f"y_last{b}", tag=f"sum{b + 2}") for b in range(QB)] if last else []
+        half_e = 2 * P
+        for h in range(2):
+            v_codes = keep.tile([P, half_e], U32, name=f"v_codes{h}", align_bytes=64)
+            v_scales = keep.tile([P, half_e], U8, name=f"v_scales{h}", align_bytes=64)
+            for g in (1,) if h == 0 else (2, 3):
+                turn_values(g, v_rows[g])
+            nc.vector.quantize_mx(v_codes[:].bitcast(FP8X4), v_scales[:], v_bf[h][:].rearrange("s e t -> s (e t)"))
             for b in range(QB):
                 cols = slice(b * P, (b + 1) * P)
-                y = y_last[b][:] if last else y_early[b][:, g * P : (g + 1) * P]
+                y = psum.tile([P, half_e], F32, name=f"y{h}_{b}", tag=f"sum{2 * h + b}")
                 nc.tensor.matmul_mx(
-                    y, w_codes[:, cols].bitcast(FP8X4), w_scales[:, cols], v_codes[:].bitcast(FP8X4), v_scales[:],
+                    y[:], w_codes[:, cols].bitcast(FP8X4), w_scales[:, cols], v_codes[:].bitcast(FP8X4), v_scales[:],
                     start=True, stop=True,
                 )
-            if g >= EB - 2:
-                e_cols = slice(early, DV) if last else slice(0, early)
-                for b in range(QB):
-                    y = y_last[b] if last else y_early[b]
-                    y_sb = keep.tile([P, P if last else early], F32, name=f"y_sb{b}_{g}")
-                    if b == 0:
-                        nc.vector.tensor_scalar(y_sb[:], y[:], inv[:, b : b + 1], None, MULT)
-                        nc.sync.dma_start(out[0, b * P : (b + 1) * P, e_cols], y_sb[:])
-                    else:
-                        nc.scalar.activation(y_sb[:], y[:], ACT.Copy, scale=inv[:, b : b + 1])
-                        (nc.scalar if last else nc.sync).dma_start(out[0, b * P : (b + 1) * P, e_cols], y_sb[:])
+                y_sb = keep.tile([P, half_e], F32, name=f"y_sb{h}_{b}")
+                if h == 1 and b == 0:
+                    nc.vector.tensor_scalar(y_sb[:], y[:], inv[:, b : b + 1], None, MULT)
+                else:
+                    nc.scalar.activation(y_sb[:], y[:], ACT.Copy, scale=inv[:, b : b + 1])
+                queue = nc.scalar if h == 1 and b == 1 else nc.sync
+                queue.dma_start(out[0, cols, h * half_e : (h + 1) * half_e], y_sb[:])

from contextlib import ExitStack

import concourse.mybir as mybir
from concourse.masks import make_identity

FLOPS = 2 * 2 * 256 * 512 * 512
BYTES = 4 * (512 * 256 + 2 * 512 * 2048 + 2 * 2048 + 256 * 512) + 2 * 128 * 32

F32 = mybir.dt.float32
BF16 = mybir.dt.bfloat16
U32 = mybir.dt.uint32
U16 = mybir.dt.uint16
U8 = mybir.dt.uint8
FP8X4 = mybir.dt.float8_e4m3fn_x4
MULT = mybir.AluOpType.mult
MIN = mybir.AluOpType.min
AXIS_X = mybir.AxisListType.X
ACT = mybir.ActivationFunctionType

P = 128
PACK = 4
T = 2048
N = 512
NQ = 256
DV = 512
QB = NQ // P
EB = DV // P
GATE = 8
SB = N // P


def tile_attend_mqa_topk_ks_kernel(tc, qT, kT, vT, ks, vs, offs, out):
    nc = tc.nc
    with ExitStack() as ctx:
        keep = ctx.enter_context(tc.tile_pool(name="keep", bufs=1))
        psum = ctx.enter_context(tc.psum_pool(name="psum", bufs=1))

        offsets = keep.tile([P, N // 16], U16, name="offsets")
        q_raw = keep.tile([P, PACK, NQ], F32, name="q_raw")
        k_win = [keep.tile([P, T], F32, name=f"k_win{t}") for t in range(PACK)]
        v_win = [keep.tile([P, T], F32, name=f"v_win{g}") for g in range(EB)]
        ks_win = keep.tile([P, T], F32, name="ks_win")
        vs_win = keep.tile([P, T], F32, name="vs_win")

        k_planes = kT.rearrange("(p j) n -> j p n", j=PACK)
        nc.sync.dma_start(offsets[:], offs)
        nc.sync.dma_start(k_win[0][:], k_planes[0])
        for win, row, split in ((vs_win, vs, 1024), (ks_win, ks, 1280)):
            nc.vector.memset(win[:, 0:split], 0.0)
            nc.gpsimd.memset(win[:, split:T], 0.0)
            nc.scalar.dma_start(win[0:1, :], row[0:1, :])
        nc.vector.memset(k_win[1][:, 0:GATE], 0.0)
        nc.sync.dma_start(k_win[1][:], k_planes[1])
        nc.vector.memset(q_raw[:, 0, 0:GATE], 0.0)
        nc.sync.dma_start(q_raw[:], qT[0].rearrange("(p j) q -> p j q", j=PACK))
        v_planes = vT.rearrange("(g e) n -> g e n", e=P)
        pool_loads = [(k_win[2], k_planes[2]), (v_win[0], v_planes[0]), (k_win[3], k_planes[3])]
        pool_loads += [(v_win[g], v_planes[g]) for g in range(1, EB)]
        for win, plane in pool_loads:
            nc.vector.memset(win[:, 0:GATE], 0.0)
            nc.sync.dma_start(win[:], plane)

        warm = keep.tile([P, 1], F32, name="warm")
        nc.vector.memset(warm[:], 0.0)
        nc.scalar.activation(warm[:], warm[:], ACT.Exp)

        ident = keep.tile([P, P], F32, name="ident")
        make_identity(nc, ident[:])

        banks = [psum.tile([P, PACK, P], F32, name=f"bank{i}") for i in range(4)]

        rows = keep.tile([P, 2, N], F32, name="rows")
        ks_row, vs_row = rows[:, 0, :], rows[:, 1, :]
        nks_col = keep.tile([P, SB], F32, name="nks_col")
        vs_col = keep.tile([P, PACK], F32, name="vs_col")
        nc.vector.tensor_copy(vs_row, vs_win[:].indirect(offsets[:]))
        vs_t = banks[1]
        for t in range(PACK):
            nc.tensor.transpose(vs_t[:, t, :], vs_row[:, t::PACK], ident[:])
        nc.vector.tensor_copy(vs_col[:], vs_t[:, :, 0])
        nc.vector.tensor_copy(ks_row, ks_win[:].indirect(offsets[:]))
        ks_t = banks[0]
        for c in range(SB):
            nc.tensor.transpose(ks_t[:, c, :], ks_row[:, c * P : (c + 1) * P], ident[:])
        nc.vector.tensor_scalar(nks_col[:], ks_t[:, :, 0], -1.0, None, MULT)

        q_bf = keep.tile([P, NQ, PACK], BF16, name="q_bf", align_bytes=64)
        q_codes = keep.tile([P, NQ], U32, name="q_codes", align_bytes=64)
        q_scales = keep.tile([P, NQ], U8, name="q_scales", align_bytes=64)
        nc.scalar.copy(q_bf[:], q_raw[:].rearrange("p j q -> p q j"))
        nc.vector.quantize_mx(q_codes[:].bitcast(FP8X4), q_scales[:], q_bf[:].rearrange("p q j -> p (q j)"))

        k_bf = keep.tile([P, N, PACK], BF16, name="k_bf", align_bytes=64)
        k_codes = keep.tile([P, N], U32, name="k_codes", align_bytes=64)
        k_scales = keep.tile([P, N], U8, name="k_scales", align_bytes=64)
        for t in range(PACK - 1):
            nc.vector.tensor_copy(k_bf[:, :, t], k_win[t][:].indirect(offsets[:]))

        v_bf = [keep.tile([P, 2 * P, PACK], BF16, name=f"v_bf{h}", align_bytes=64) for h in range(2)]
        v_row0 = keep.tile([P, N], F32, name="v_row0")

        def turn_values(g, row):
            v_t = banks[(g + 2) % 4]
            for t in range(PACK):
                nc.tensor.transpose(v_t[:, t, :], row[:, t::PACK], ident[:])
            e_cols = slice((g % 2) * P, (g % 2 + 1) * P)
            nc.scalar.copy(v_bf[g // 2][:, e_cols, :], v_t[:].rearrange("s t e -> s e t"))

        nc.vector.tensor_copy(v_row0[:], v_win[0][:].indirect(offsets[:]))
        turn_values(0, v_row0)

        nc.vector.tensor_copy(k_bf[:, :, PACK - 1], k_win[PACK - 1][:].indirect(offsets[:]))
        half = N // 2
        for h in range(2):
            cols = slice(h * half, (h + 1) * half)
            nc.vector.quantize_mx(
                k_codes[:, cols].bitcast(FP8X4), k_scales[:, cols], k_bf[:, cols, :].rearrange("p n j -> p (n j)")
            )

        a_t = keep.tile([P, SB, NQ], F32, name="a_t")
        for c in range(SB):
            cols = slice(c * P, (c + 1) * P)
            score = psum.tile([P, NQ], F32, name=f"score{c}", tag=f"sum{c}")
            nc.tensor.matmul_mx(
                score[:], k_codes[:, cols].bitcast(FP8X4), k_scales[:, cols], q_codes[:].bitcast(FP8X4), q_scales[:],
                start=True, stop=True,
            )
            nc.scalar.activation(a_t[:, c, :], score[:], ACT.Copy, scale=nks_col[:, c : c + 1])

        neg_m = keep.tile([P, QB], F32, name="neg_m")
        total = [keep.tile([P, 1], F32, name=f"total{b}") for b in range(QB)]
        inv = keep.tile([P, QB], F32, name="inv")
        w_codes = keep.tile([P, NQ], U32, name="w_codes", align_bytes=64)
        w_scales = keep.tile([P, NQ], U8, name="w_scales", align_bytes=64)
        a_q = []
        for b in range(QB):
            a_b = banks[b]
            for c in range(SB):
                nc.tensor.transpose(a_b[:, c, :], a_t[:, c, b * P : (b + 1) * P], ident[:])
            a_q.append(a_b)
        p_sb = []
        for b in range(QB):
            nc.vector.tensor_reduce(neg_m[:, b : b + 1], a_q[b][:].rearrange("q c s -> q (c s)"), AXIS_X, MIN)
            p_b = keep.tile([P, PACK, P], F32, name=f"p_sb{b}")
            nc.scalar.activation(
                p_b[:], a_q[b][:].rearrange("q c s -> q (c s)").rearrange("q (s t) -> q t s", t=PACK), ACT.Exp,
                bias=neg_m[:, b : b + 1], scale=-1.0, accum_out=total[b][:],
            )
            p_sb.append(p_b)
        for b in range(QB):
            p_t = banks[b + 2]
            for t in range(PACK):
                nc.tensor.transpose(p_t[:, t, :], p_sb[b][:, t, :], ident[:])
            w_bf = keep.tile([P, P, PACK], BF16, name=f"w_bf{b}", align_bytes=64)
            nc.vector.tensor_tensor(
                w_bf[:], p_t[:].rearrange("s t q -> s q t"),
                vs_col[:].unsqueeze(1).to_broadcast([P, P, PACK]), MULT,
            )
            cols = slice(b * P, (b + 1) * P)
            nc.vector.quantize_mx(
                w_codes[:, cols].bitcast(FP8X4), w_scales[:, cols], w_bf[:].rearrange("s q t -> s (q t)")
            )
            nc.vector.reciprocal(inv[:, b : b + 1], total[b][:])

        v_rows = [
            v_row0[:],
            a_t[:, 2:4, :].rearrange("s c q -> s (c q)"),
            p_sb[1][:].rearrange("q t s -> q (t s)"),
            p_sb[0][:].rearrange("q t s -> q (t s)"),
        ]
        for g in range(1, EB):
            nc.vector.tensor_copy(v_rows[g], v_win[g][:].indirect(offsets[:]))
        half_e = 2 * P
        for h in range(2):
            v_codes = keep.tile([P, half_e], U32, name=f"v_codes{h}", align_bytes=64)
            v_scales = keep.tile([P, half_e], U8, name=f"v_scales{h}", align_bytes=64)
            for g in (1,) if h == 0 else (2, 3):
                turn_values(g, v_rows[g])
            nc.vector.quantize_mx(v_codes[:].bitcast(FP8X4), v_scales[:], v_bf[h][:].rearrange("s e t -> s (e t)"))
            for b in range(QB):
                cols = slice(b * P, (b + 1) * P)
                y = psum.tile([P, half_e], F32, name=f"y{h}_{b}", tag=f"sum{2 * h + b}")
                nc.tensor.matmul_mx(
                    y[:], w_codes[:, cols].bitcast(FP8X4), w_scales[:, cols], v_codes[:].bitcast(FP8X4), v_scales[:],
                    start=True, stop=True,
                )
                y_sb = keep.tile([P, half_e], F32, name=f"y_sb{h}_{b}")
                if h == 1 and b == 0:
                    nc.vector.tensor_scalar(y_sb[:], y[:], inv[:, b : b + 1], None, MULT)
                else:
                    nc.scalar.activation(y_sb[:], y[:], ACT.Copy, scale=inv[:, b : b + 1])
                queue = nc.scalar if h == 1 and b == 1 else nc.sync
                queue.dma_start(out[0, cols, h * half_e : (h + 1) * half_e], y_sb[:])
